import numpy as np
import ml_dtypes


def mxq(x, axis, fmt="e4m3"):
    dtype, down = {"e4m3": (ml_dtypes.float8_e4m3fn, 7), "e5m2": (ml_dtypes.float8_e5m2, 14)}[fmt]
    v = np.moveaxis(np.asarray(x, np.float32).astype(ml_dtypes.bfloat16).astype(np.float64), axis, -1)
    blocks = v.reshape(v.shape[:-1] + (-1, 32))
    amax = np.abs(blocks).max(-1, keepdims=True)
    byte = np.maximum(np.where(amax > 0, np.frexp(amax)[1] - 1 + 127, 0) - down, 1)
    scale = np.exp2(byte - 127.0)
    codes = (blocks / scale).astype(np.float32).astype(dtype).astype(np.float64)
    return np.moveaxis((codes * scale).reshape(v.shape), -1, axis)


WIDE = False


def mx_kscale(k):
    if not WIDE:
        return np.ones(k)
    levels = np.array([10, -10, 5, -5, 0])
    if k % 512:
        return np.exp2(np.random.permutation(np.resize(levels, k // 32))).repeat(32)
    a = np.empty((k // 512, 16))
    for p in range(k // 512):
        a[p, :8] = np.random.permutation(np.resize(levels, 8))
        for g in range(8):
            far = levels[np.abs(levels - a[p, g]) >= 10]
            a[p, g + 8] = far[np.random.randint(len(far))]
    return np.exp2(a.ravel()).repeat(32)


def f64(x):
    return np.asarray(x).astype(np.float64)


def striped(idx):
    return np.tile(idx.reshape(-1, 16).T, (8, 1)).astype(np.uint16)


def unstriped(offs):
    return offs[:16].T.reshape(-1).astype(np.int64)


def pack_weight(w):
    k, n = w.shape
    w = f64(np.asarray(w, np.float32).astype(ml_dtypes.bfloat16)).reshape(k // 32, 32, n)
    amax = np.abs(w).max(1)
    byte = np.clip(np.where(amax > 0, np.frexp(amax)[1] - 1 + 127 - 7, 1), 1, 254)
    scaled = (w * np.exp2(127.0 - byte)[:, None, :]).reshape(k, n).astype(np.float32)
    words = np.ascontiguousarray(scaled.reshape(k // 512, 128, 4, n).transpose(0, 1, 3, 2)).astype(ml_dtypes.float8_e4m3fn).view(np.uint8)
    return words, np.ascontiguousarray(byte.astype(np.uint8).reshape(k // 512, 16, n))


def unpack_weight(words, scales):
    g, p, n, _ = words.shape
    vals = np.ascontiguousarray(words).view(ml_dtypes.float8_e4m3fn).astype(np.float64) * np.repeat(np.exp2(scales.astype(np.float64) - 127.0), 8, axis=1)[..., None]
    return vals.transpose(0, 1, 3, 2).reshape(g * 512, n)


def relu(v):
    return np.maximum(v, 0.0)


K, T, S, H, N, D = 512, 4096, 1024, 512, 128, 2


def setup_inputs():
    n = np.random.standard_normal
    s = mx_kscale(K)[:, None]
    u = mx_kscale(H)
    packed_xT = pack_weight(n((K, T)) * s)
    return {
        "x_words": packed_xT[0],
        "x_scales": packed_xT[1],
        "w1": (n((K, H)) / np.sqrt(K) / s).astype(np.float32),
        "w2": (n((H, N)) / np.sqrt(H) / u[:, None]).astype(np.float32),
        "gain": (np.random.uniform(0.5, 1.5, (H, 1)) * u[:, None]).astype(np.float32),
        "offs": striped(np.random.permutation(T)[:S]),
    }


def reference(x_words, x_scales, w1, w2, gain, offs):
    xq = unpack_weight(x_words, x_scales)[:, unstriped(offs)]
    y = relu(mxq(f64(w1), 0, "e4m3").T @ xq) + 0.05
    ee = (y * y) * y
    z = f64(gain) * (np.exp((np.log(ee.reshape(len(ee), -1, D).mean(axis=2))) / 3))
    return np.tanh(mxq(f64(w2), 0, "e4m3").T @ mxq(z, 0, "e4m3"))

@@ -1,0 +1,183 @@
+from contextlib import ExitStack
+
+import concourse.mybir as mybir
+
+K, T, S, H, N, D = 512, 4096, 1024, 512, 128, 2
+V = S // D
+FLOPS = 2 * K * H * S + 2 * H * N * V
+
+F32 = mybir.dt.float32
+BF16 = mybir.dt.bfloat16
+I32 = mybir.dt.int32
+U32 = mybir.dt.uint32
+U16 = mybir.dt.uint16
+U8 = mybir.dt.uint8
+FP8X4 = mybir.dt.float8_e4m3fn_x4
+ALU = mybir.AluOpType
+ACT = mybir.ActivationFunctionType
+
+P = 128
+PACK = 4
+HALF = 512
+PAIRS = HALF // D
+FLOOR = 0.05
+LN_SMALLEST = 2.0**-64
+F32_LARGEST = (2.0 - 2.0**-23) * 2.0**127
+CUBE_GROUPS = (((0, 1), (2, 3)), ((0, 1), (2,), (3,)))
+IMAGE_CHUNKS = ((0, 256), (256, 384), (384, 448), (448, 512))
+SHIFT_WIDTH = 128
+
+
+def tile_picked_ygem_tanh_p_kernel(tc, x_words, x_scales, w1, w2, gain, offs, out):
+    nc = tc.nc
+    with ExitStack() as ctx:
+        keep = ctx.enter_context(tc.tile_pool(name="keep", bufs=1))
+        ring = ctx.enter_context(tc.tile_pool(name="ring", bufs=3))
+        psum = ctx.enter_context(tc.psum_pool(name="psum", bufs=8))
+
+        offsets = keep.tile([P, S // 16], U16, name="offsets")
+        nc.sync.dma_start(offsets[:], offs)
+        gain_raw = keep.tile([P, PACK], F32, name="gain_raw")
+        nc.scalar.dma_start(gain_raw[:], gain.rearrange("(p t) o -> p (t o)", t=PACK))
+        scale_table = keep.tile([P, T], U8, name="scale_table", align_bytes=64)
+        nc.vector.memset(scale_table[:].bitcast(I32), 0)
+        w1_raw = keep.tile([P, PACK, H], F32, name="w1_raw")
+        w1_rows = w1.rearrange("(p j) c -> p j c", j=PACK)
+        nc.sync.dma_start(w1_raw[:, 0:2, :], w1_rows[:, 0:2, :])
+        nc.sync.dma_start(scale_table[0:P:8, :].bitcast(I32), x_scales[0].bitcast(I32))
+        nc.sync.dma_start(w1_raw[:, 2:4, :], w1_rows[:, 2:4, :])
+        word_table = keep.tile([P, T], U32, name="word_table", align_bytes=64)
+        nc.sync.dma_start(word_table[:].bitcast(I32), x_words[0].rearrange("p n r -> p (n r)").bitcast(I32))
+        w2_raw = keep.tile([P, PACK, N], F32, name="w2_raw")
+        nc.sync.dma_start(w2_raw[:], w2.rearrange("(p t) n -> p t n", t=PACK))
+
+        gain_abs = keep.tile([P, PACK], F32, name="gain_abs")
+        nc.vector.scalar_tensor_tensor(gain_abs[:], gain_raw[:], -1.0, gain_raw[:], ALU.mult, ALU.max)
+        gain_clamped = keep.tile([P, PACK], F32, name="gain_clamped")
+        nc.vector.tensor_scalar_max(gain_clamped[:], gain_abs[:], LN_SMALLEST)
+        gain_log = keep.tile([P, PACK], F32, name="gain_log")
+        nc.scalar.activation(gain_log[:], gain_clamped[:], ACT.Ln)
+        gain_log3 = keep.tile([P, PACK], F32, name="gain_log3")
+        nc.vector.tensor_scalar(gain_log3[:], gain_log[:], 3.0, None, ALU.mult)
+        gain_step = keep.tile([P, PACK], F32, name="gain_step")
+        nc.vector.tensor_scalar(gain_step[:], gain_raw[:], 0.0, 2.0, ALU.is_ge, ALU.mult)
+        gain_sign = keep.tile([P, PACK], BF16, name="gain_sign")
+        nc.vector.tensor_scalar(gain_sign[:], gain_step[:], -1.0, None, ALU.add)
+
+        x_scale_rows = keep.tile([P, S], U8, name="x_scale_rows", align_bytes=64)
+        nc.vector.memset(x_scale_rows[:].bitcast(I32), 0)
+        picked_scales = keep.tile([P, S], U8, name="picked_scales", align_bytes=64)
+        nc.vector.tensor_copy(picked_scales[:], scale_table[:].indirect(offsets[:]))
+        for q in range(4):
+            nc.scalar.dma_start(
+                x_scale_rows[32 * q : 32 * q + 4, :].bitcast(I32),
+                picked_scales[32 * q : 32 * q + 32 : 8, :].bitcast(I32),
+            )
+
+        w1_grouped = keep.tile([P, PACK * H], BF16, name="w1_grouped", align_bytes=64)
+        nc.vector.tensor_copy(
+            w1_grouped[:].rearrange("p (t c m j) -> p c j m t", t=PACK, m=2, j=PACK),
+            w1_raw[:].rearrange("p j (c m t) -> p c j m t", m=2, t=PACK),
+        )
+        w1_codes = keep.tile([P, H], U32, name="w1_codes", align_bytes=64)
+        w1_scales = keep.tile([P, H], U8, name="w1_scales", align_bytes=64)
+        nc.vector.quantize_mx(w1_codes[:].bitcast(FP8X4), w1_scales[:], w1_grouped[:])
+
+        picked_words = []
+        for h in range(2):
+            words = keep.tile([P, HALF], U32, name="picked_words%d" % h, align_bytes=64)
+            nc.vector.tensor_copy(words[:], word_table[:].indirect(offsets[:, 32 * h : 32 * (h + 1)]))
+            picked_words.append(words)
+
+        w2_grouped = keep.tile([P, N, PACK], BF16, name="w2_grouped", align_bytes=64)
+        nc.scalar.copy(
+            w2_grouped[:].rearrange("p (c i) t -> p c t i", i=4),
+            w2_raw[:].rearrange("p t (c i) -> p c t i", i=4),
+        )
+
+        cube_sums = keep.tile([P, 2, PACK, PAIRS], F32, name="cube_sums", tag="sums_then_z", align_bytes=64)
+        logs = [keep.tile([P, PACK, PAIRS], F32, name="logs%d" % h, align_bytes=64) for h in range(2)]
+
+        def cube(h, t, first, second, v0, v1, by_member_apart):
+            acc = psum.tile([P, D * (v1 - v0)], F32, name="acc", tag="bank")
+            nc.tensor.matmul_mx(
+                acc[:],
+                lhsT=w1_codes[:, P * t : P * (t + 1)].bitcast(FP8X4),
+                lhsT_scale=w1_scales[:, P * t : P * (t + 1)],
+                rhs=picked_words[h][:, D * v0 : D * v1].bitcast(FP8X4),
+                rhs_scale=x_scale_rows[:, HALF * h + D * v0 : HALF * h + D * v1],
+                start=True,
+                stop=True,
+            )
+            by_member = acc[:].rearrange("p (v d) -> p d v", d=D)
+            square = ring.tile([P, D, v1 - v0], F32, name="square")
+            nc.scalar.activation(square[:], by_member, ACT.Square, bias=1.5 * FLOOR)
+            lifted = first[:, :, v0:v1]
+            if by_member_apart:
+                for d in (1, 0):
+                    nc.vector.scalar_tensor_tensor(
+                        lifted[:, d, :], square[:, d, :], 0.75 * FLOOR * FLOOR, by_member[:, d, :], ALU.add, ALU.mult
+                    )
+            else:
+                nc.vector.scalar_tensor_tensor(lifted, square[:], 0.75 * FLOOR * FLOOR, by_member, ALU.add, ALU.mult)
+            nc.gpsimd.tensor_scalar(second[:, v0:v1], lifted[:, 1, :], F32_LARGEST, 0.0, ALU.min, ALU.max)
+
+        def pool_pairs(h, group, lifted, second):
+            rows = slice(group[0], group[-1] + 1)
+            nc.vector.scalar_tensor_tensor(cube_sums[:, h, rows, :], lifted[:, :, 0, :], 0.0, second[:], ALU.max, ALU.add)
+            nc.scalar.activation(logs[h][:, rows, :], cube_sums[:, h, rows, :], ACT.Ln, scale=1.0 / D, bias=FLOOR**3)
+
+        pending = []
+        for h in range(2):
+            for group in CUBE_GROUPS[h]:
+                lifted = ring.tile([P, len(group), D, PAIRS], F32, name="lifted")
+                second = ring.tile([P, len(group), PAIRS], F32, name="second")
+                for i, t in enumerate(group):
+                    cuts = (0, PAIRS // 2, PAIRS) if (h, t) == (0, 0) else (0, PAIRS)
+                    for v0, v1 in zip(cuts, cuts[1:]):
+                        cube(h, t, lifted[:, i, :, :], second[:, i, :], v0, v1, (h, t) == (1, PACK - 1))
+                    if pending:
+                        pool_pairs(*pending.pop())
+                pending.append((h, group, lifted, second))
+        pool_pairs(*pending.pop())
+
+        w2_codes = keep.tile([P, N], U32, name="w2_codes", align_bytes=64)
+        w2_scales = keep.tile([P, N], U8, name="w2_scales", align_bytes=64)
+        w2_signed = keep.tile([P, N, PACK], BF16, name="w2_signed", align_bytes=64)
+        nc.vector.tensor_tensor(w2_signed[:], w2_grouped[:], gain_sign[:].unsqueeze(1).to_broadcast([P, N, PACK]), ALU.mult)
+        nc.vector.quantize_mx(w2_codes[:].bitcast(FP8X4), w2_scales[:], w2_signed[:].rearrange("p n t -> p (n t)"))
+
+        z = keep.tile([P, V * PACK], BF16, name="z", tag="sums_then_z", align_bytes=64)
+        z_codes = keep.tile([P, V], U32, name="z_codes", align_bytes=64)
+        z_scales = keep.tile([P, V], U8, name="z_scales", align_bytes=64)
+        products = []
+        for v0, v1 in IMAGE_CHUNKS:
+            shifted = keep.tile([P, (v1 - v0) * PACK], F32, name="shifted%d" % v0, align_bytes=64)
+            for a in range(v0, v1, SHIFT_WIDTH):
+                b = min(a + SHIFT_WIDTH, v1)
+                h, a_in_half = divmod(a, PAIRS)
+                runs = (b - a) // 4
+                nc.vector.tensor_tensor(
+                    shifted[:, (a - v0) * PACK : (b - v0) * PACK].rearrange("p (c i t) -> p c t i", i=4, t=PACK),
+                    logs[h][:, :, a_in_half : a_in_half + b - a].rearrange("p t (c i) -> p c t i", i=4),
+                    gain_log3[:].unsqueeze(1).unsqueeze(3).to_broadcast([P, runs, PACK, 4]),
+                    ALU.add,
+                )
+            nc.scalar.activation(z[:, v0 * PACK : v1 * PACK], shifted[:], ACT.Exp, scale=1.0 / 3.0)
+        for v0, v1 in IMAGE_CHUNKS:
+            nc.vector.quantize_mx(z_codes[:, v0:v1].bitcast(FP8X4), z_scales[:, v0:v1], z[:, v0 * PACK : v1 * PACK])
+            product = psum.tile([P, v1 - v0], F32, name="product", tag="bank")
+            nc.tensor.matmul_mx(
+                product[:],
+                lhsT=w2_codes[:].bitcast(FP8X4),
+                lhsT_scale=w2_scales[:],
+                rhs=z_codes[:, v0:v1].bitcast(FP8X4),
+                rhs_scale=z_scales[:, v0:v1],
+                start=True,
+                stop=True,
+            )
+            products.append(product)
+        for (v0, v1), product in zip(IMAGE_CHUNKS, products):
+            result = keep.tile([P, v1 - v0], F32, name="result%d" % v0)
+            nc.scalar.activation(result[:], product[:], ACT.Tanh)
+            nc.sync.dma_start(out[:, v0:v1], result[:])

@@ -19,11 +19,12 @@ ACT = mybir.ActivationFunctionType
 P = 128
 PACK = 4
 HALF = 512
-PAIRS = HALF // D
 FLOOR = 0.05
 LN_SMALLEST = 2.0**-64
-F32_LARGEST = (2.0 - 2.0**-23) * 2.0**127
-CUBE_GROUPS = (((0, 1), (2, 3)), ((0, 1), (2,), (3,)))
+BANK_ENTRIES = 128
+BANK_IMAGES = BANK_ENTRIES // D
+BANK_COLS = BANK_IMAGES * PACK
+BANK_GROUPS = (((0, 1), False), ((2, 3), True), ((4, 5), True), ((6,), False), ((7,), False))
 IMAGE_CHUNKS = ((0, 256), (256, 384), (384, 448), (448, 512))
 SHIFT_WIDTH = 128
 
@@ -32,7 +33,6 @@ def tile_picked_ygem_tanh_p_kernel(tc, x_words, x_scales, w1, w2, gain, offs, ou
     nc = tc.nc
     with ExitStack() as ctx:
         keep = ctx.enter_context(tc.tile_pool(name="keep", bufs=1))
-        ring = ctx.enter_context(tc.tile_pool(name="ring", bufs=3))
         psum = ctx.enter_context(tc.psum_pool(name="psum", bufs=8))
 
         offsets = keep.tile([P, S // 16], U16, name="offsets")
@@ -95,50 +95,59 @@ def tile_picked_ygem_tanh_p_kernel(tc, x_words, x_scales, w1, w2, gain, offs, ou
             w2_raw[:].rearrange("p t (c i) -> p c t i", i=4),
         )
 
-        cube_sums = keep.tile([P, 2, PACK, PAIRS], F32, name="cube_sums", tag="sums_then_z", align_bytes=64)
-        logs = [keep.tile([P, PACK, PAIRS], F32, name="logs%d" % h, align_bytes=64) for h in range(2)]
+        cube_sums = keep.tile([P, V * PACK], F32, name="cube_sums", tag="sums_then_z", align_bytes=64)
+        logs = keep.tile([P, V * PACK], F32, name="logs", align_bytes=64)
 
-        def cube(h, t, first, second, v0, v1, by_member_apart):
-            acc = psum.tile([P, D * (v1 - v0)], F32, name="acc", tag="bank")
-            nc.tensor.matmul_mx(
-                acc[:],
-                lhsT=w1_codes[:, P * t : P * (t + 1)].bitcast(FP8X4),
-                lhsT_scale=w1_scales[:, P * t : P * (t + 1)],
-                rhs=picked_words[h][:, D * v0 : D * v1].bitcast(FP8X4),
-                rhs_scale=x_scale_rows[:, HALF * h + D * v0 : HALF * h + D * v1],
-                start=True,
-                stop=True,
-            )
-            by_member = acc[:].rearrange("p (v d) -> p d v", d=D)
-            square = ring.tile([P, D, v1 - v0], F32, name="square")
+        def cube(bank, lifted):
+            h, first = divmod(bank * BANK_ENTRIES, HALF)
+            acc = psum.tile([P, PACK, BANK_ENTRIES], F32, name="acc", tag="bank")
+            for t in range(PACK):
+                nc.tensor.matmul_mx(
+                    acc[:, t, :],
+                    lhsT=w1_codes[:, P * t : P * (t + 1)].bitcast(FP8X4),
+                    lhsT_scale=w1_scales[:, P * t : P * (t + 1)],
+                    rhs=picked_words[h][:, first : first + BANK_ENTRIES].bitcast(FP8X4),
+                    rhs_scale=x_scale_rows[:, bank * BANK_ENTRIES : (bank + 1) * BANK_ENTRIES],
+                    start=True,
+                    stop=True,
+                )
+            by_member = acc[:].rearrange("p t (v d) -> p d v t", d=D)
+            square = keep.tile([P, D, BANK_IMAGES, PACK], F32, name="square%d" % bank)
             nc.scalar.activation(square[:], by_member, ACT.Square, bias=1.5 * FLOOR)
-            lifted = first[:, :, v0:v1]
-            if by_member_apart:
-                for d in (1, 0):
-                    nc.vector.scalar_tensor_tensor(
-                        lifted[:, d, :], square[:, d, :], 0.75 * FLOOR * FLOOR, by_member[:, d, :], ALU.add, ALU.mult
-                    )
-            else:
-                nc.vector.scalar_tensor_tensor(lifted, square[:], 0.75 * FLOOR * FLOOR, by_member, ALU.add, ALU.mult)
-            nc.gpsimd.tensor_scalar(second[:, v0:v1], lifted[:, 1, :], F32_LARGEST, 0.0, ALU.min, ALU.max)
+            for d in (1, 0):
+                nc.vector.scalar_tensor_tensor(
+                    lifted[:, d, :].rearrange("p (v t) -> p v t", t=PACK),
+                    square[:, d, :, :],
+                    0.75 * FLOOR * FLOOR,
+                    by_member[:, d, :, :],
+                    ALU.add,
+                    ALU.mult,
+                )
 
-        def pool_pairs(h, group, lifted, second):
-            rows = slice(group[0], group[-1] + 1)
-            nc.vector.scalar_tensor_tensor(cube_sums[:, h, rows, :], lifted[:, :, 0, :], 0.0, second[:], ALU.max, ALU.add)
-            nc.scalar.activation(logs[h][:, rows, :], cube_sums[:, h, rows, :], ACT.Ln, scale=1.0 / D, bias=FLOOR**3)
+        def clamp(group, on_scalar, lifted):
+            second = keep.tile([P, len(group), BANK_COLS], F32, name="second%d" % group[0])
+            if on_scalar:
+                nc.scalar.activation(second[:], lifted[:, :, 1, :], ACT.Relu)
+            else:
+                nc.vector.tensor_scalar_max(second[:], lifted[:, :, 1, :], 0.0)
+            return second
+
+        def pool_pairs(group, lifted, second):
+            cols = slice(group[0] * BANK_COLS, (group[-1] + 1) * BANK_COLS)
+            sums = cube_sums[:, cols].rearrange("p (g c) -> p g c", c=BANK_COLS)
+            nc.vector.scalar_tensor_tensor(sums, lifted[:, :, 0, :], 0.0, second[:], ALU.max, ALU.add)
+            nc.scalar.activation(logs[:, cols], cube_sums[:, cols], ACT.Ln, scale=1.0 / D, bias=FLOOR**3)
 
         pending = []
-        for h in range(2):
-            for group in CUBE_GROUPS[h]:
-                lifted = ring.tile([P, len(group), D, PAIRS], F32, name="lifted")
-                second = ring.tile([P, len(group), PAIRS], F32, name="second")
-                for i, t in enumerate(group):
-                    cuts = (0, PAIRS // 2, PAIRS) if (h, t) == (0, 0) else (0, PAIRS)
-                    for v0, v1 in zip(cuts, cuts[1:]):
-                        cube(h, t, lifted[:, i, :, :], second[:, i, :], v0, v1, (h, t) == (1, PACK - 1))
-                    if pending:
-                        pool_pairs(*pending.pop())
-                pending.append((h, group, lifted, second))
+        for group, on_scalar in BANK_GROUPS:
+            lifted = keep.tile([P, len(group), D, BANK_COLS], F32, name="lifted%d" % group[0])
+            for i, bank in enumerate(group):
+                cube(bank, lifted[:, i, :, :])
+                if bank == group[-1]:
+                    second = clamp(group, on_scalar, lifted)
+                if pending:
+                    pool_pairs(*pending.pop())
+            pending.append((group, lifted, second))
         pool_pairs(*pending.pop())
 
         w2_codes = keep.tile([P, N], U32, name="w2_codes", align_bytes=64)
@@ -151,19 +160,17 @@ def tile_picked_ygem_tanh_p_kernel(tc, x_words, x_scales, w1, w2, gain, offs, ou
         z_codes = keep.tile([P, V], U32, name="z_codes", align_bytes=64)
         z_scales = keep.tile([P, V], U8, name="z_scales", align_bytes=64)
         products = []
+        shifted = keep.tile([P, V * PACK], F32, name="shifted", tag="shifted_then_result", align_bytes=64)
         for v0, v1 in IMAGE_CHUNKS:
-            shifted = keep.tile([P, (v1 - v0) * PACK], F32, name="shifted%d" % v0, align_bytes=64)
             for a in range(v0, v1, SHIFT_WIDTH):
                 b = min(a + SHIFT_WIDTH, v1)
-                h, a_in_half = divmod(a, PAIRS)
-                runs = (b - a) // 4
                 nc.vector.tensor_tensor(
-                    shifted[:, (a - v0) * PACK : (b - v0) * PACK].rearrange("p (c i t) -> p c t i", i=4, t=PACK),
-                    logs[h][:, :, a_in_half : a_in_half + b - a].rearrange("p t (c i) -> p c t i", i=4),
-                    gain_log3[:].unsqueeze(1).unsqueeze(3).to_broadcast([P, runs, PACK, 4]),
+                    shifted[:, a * PACK : b * PACK].rearrange("p (v t) -> p v t", t=PACK),
+                    logs[:, a * PACK : b * PACK].rearrange("p (v t) -> p v t", t=PACK),
+                    gain_log3[:].unsqueeze(1).to_broadcast([P, b - a, PACK]),
                     ALU.add,
                 )
-            nc.scalar.activation(z[:, v0 * PACK : v1 * PACK], shifted[:], ACT.Exp, scale=1.0 / 3.0)
+            nc.scalar.activation(z[:, v0 * PACK : v1 * PACK], shifted[:, v0 * PACK : v1 * PACK], ACT.Exp, scale=1.0 / 3.0)
         for v0, v1 in IMAGE_CHUNKS:
             nc.vector.quantize_mx(z_codes[:, v0:v1].bitcast(FP8X4), z_scales[:, v0:v1], z[:, v0 * PACK : v1 * PACK])
             product = psum.tile([P, v1 - v0], F32, name="product", tag="bank")
@@ -177,7 +184,8 @@ def tile_picked_ygem_tanh_p_kernel(tc, x_words, x_scales, w1, w2, gain, offs, ou
                 stop=True,
             )
             products.append(product)
+        result = keep.tile([P, V], F32, name="result", tag="shifted_then_result", align_bytes=64)
         for (v0, v1), product in zip(IMAGE_CHUNKS, products):
-            result = keep.tile([P, v1 - v0], F32, name="result%d" % v0)
-            nc.scalar.activation(result[:], product[:], ACT.Tanh)
-            nc.sync.dma_start(out[:, v0:v1], result[:])
+            nc.scalar.activation(result[:, v0:v1], product[:], ACT.Tanh)
+            queue = nc.scalar if v1 == V else nc.sync
+            queue.dma_start(out[:, v0:v1], result[:, v0:v1])

@@ -26,7 +26,8 @@ BANK_IMAGES = BANK_ENTRIES // D
 BANK_COLS = BANK_IMAGES * PACK
 BANK_GROUPS = (((0, 1), False), ((2, 3), True), ((4, 5), True), ((6,), False), ((7,), False))
 IMAGE_CHUNKS = ((0, 256), (256, 384), (384, 448), (448, 512))
-SHIFT_WIDTH = 128
+EXP_PIECES = ((0, 16), (16, 256), (256, 384), (384, 448), (448, 512))
+SHIFT_PIECES = ((16, 256), (256, 384), (384, 448), (448, 512))
 
 
 def tile_picked_ygem_tanh_p_kernel(tc, x_words, x_scales, w1, w2, gain, offs, out):
@@ -36,20 +37,18 @@ def tile_picked_ygem_tanh_p_kernel(tc, x_words, x_scales, w1, w2, gain, offs, ou
         psum = ctx.enter_context(tc.psum_pool(name="psum", bufs=8))
 
         offsets = keep.tile([P, S // 16], U16, name="offsets")
-        nc.sync.dma_start(offsets[:], offs)
         gain_raw = keep.tile([P, PACK], F32, name="gain_raw")
         nc.scalar.dma_start(gain_raw[:], gain.rearrange("(p t) o -> p (t o)", t=PACK))
         scale_table = keep.tile([P, T], U8, name="scale_table", align_bytes=64)
         nc.vector.memset(scale_table[:].bitcast(I32), 0)
-        w1_raw = keep.tile([P, PACK, H], F32, name="w1_raw")
+        w1_raw = keep.tile([P, PACK, H], F32, name="w1_raw", tag="w1_then_w2")
         w1_rows = w1.rearrange("(p j) c -> p j c", j=PACK)
         nc.sync.dma_start(w1_raw[:, 0:2, :], w1_rows[:, 0:2, :])
+        nc.sync.dma_start(offsets[:], offs)
         nc.sync.dma_start(scale_table[0:P:8, :].bitcast(I32), x_scales[0].bitcast(I32))
         nc.sync.dma_start(w1_raw[:, 2:4, :], w1_rows[:, 2:4, :])
         word_table = keep.tile([P, T], U32, name="word_table", align_bytes=64)
         nc.sync.dma_start(word_table[:].bitcast(I32), x_words[0].rearrange("p n r -> p (n r)").bitcast(I32))
-        w2_raw = keep.tile([P, PACK, N], F32, name="w2_raw")
-        nc.sync.dma_start(w2_raw[:], w2.rearrange("(p t) n -> p t n", t=PACK))
 
         gain_abs = keep.tile([P, PACK], F32, name="gain_abs")
         nc.vector.scalar_tensor_tensor(gain_abs[:], gain_raw[:], -1.0, gain_raw[:], ALU.mult, ALU.max)
@@ -69,16 +68,16 @@ def tile_picked_ygem_tanh_p_kernel(tc, x_words, x_scales, w1, w2, gain, offs, ou
         picked_scales = keep.tile([P, S], U8, name="picked_scales", align_bytes=64)
         nc.vector.tensor_copy(picked_scales[:], scale_table[:].indirect(offsets[:]))
         for q in range(4):
-            nc.scalar.dma_start(
+            nc.sync.dma_start(
                 x_scale_rows[32 * q : 32 * q + 4, :].bitcast(I32),
                 picked_scales[32 * q : 32 * q + 32 : 8, :].bitcast(I32),
             )
 
         w1_grouped = keep.tile([P, PACK * H], BF16, name="w1_grouped", align_bytes=64)
-        nc.vector.tensor_copy(
-            w1_grouped[:].rearrange("p (t c m j) -> p c j m t", t=PACK, m=2, j=PACK),
-            w1_raw[:].rearrange("p j (c m t) -> p c j m t", m=2, t=PACK),
-        )
+        w1_to = w1_grouped[:].rearrange("p (t m j) -> p m t j", t=PACK, j=PACK)
+        w1_from = w1_raw[:].rearrange("p j (m t) -> p m t j", t=PACK)
+        nc.vector.tensor_copy(w1_to[:, :, 0:2, :], w1_from[:, :, 0:2, :])
+        nc.scalar.copy(w1_to[:, :, 2:4, :], w1_from[:, :, 2:4, :])
         w1_codes = keep.tile([P, H], U32, name="w1_codes", align_bytes=64)
         w1_scales = keep.tile([P, H], U8, name="w1_scales", align_bytes=64)
         nc.vector.quantize_mx(w1_codes[:].bitcast(FP8X4), w1_scales[:], w1_grouped[:])
@@ -89,6 +88,8 @@ def tile_picked_ygem_tanh_p_kernel(tc, x_words, x_scales, w1, w2, gain, offs, ou
             nc.vector.tensor_copy(words[:], word_table[:].indirect(offsets[:, 32 * h : 32 * (h + 1)]))
             picked_words.append(words)
 
+        w2_raw = keep.tile([P, PACK, N], F32, name="w2_raw", tag="w1_then_w2")
+        nc.sync.dma_start(w2_raw[:], w2.rearrange("(p t) n -> p t n", t=PACK))
         w2_grouped = keep.tile([P, N, PACK], BF16, name="w2_grouped", align_bytes=64)
         nc.scalar.copy(
             w2_grouped[:].rearrange("p (c i) t -> p c t i", i=4),
@@ -96,7 +97,7 @@ def tile_picked_ygem_tanh_p_kernel(tc, x_words, x_scales, w1, w2, gain, offs, ou
         )
 
         cube_sums = keep.tile([P, V * PACK], F32, name="cube_sums", tag="sums_then_z", align_bytes=64)
-        logs = keep.tile([P, V * PACK], F32, name="logs", align_bytes=64)
+        logs = keep.tile([P, V * PACK], F32, name="logs", tag="logs_then_codes", align_bytes=64)
 
         def cube(bank, lifted):
             h, first = divmod(bank * BANK_ENTRIES, HALF)
@@ -132,11 +133,26 @@ def tile_picked_ygem_tanh_p_kernel(tc, x_words, x_scales, w1, w2, gain, offs, ou
                 nc.vector.tensor_scalar_max(second[:], lifted[:, :, 1, :], 0.0)
             return second
 
-        def pool_pairs(group, lifted, second):
-            cols = slice(group[0] * BANK_COLS, (group[-1] + 1) * BANK_COLS)
-            sums = cube_sums[:, cols].rearrange("p (g c) -> p g c", c=BANK_COLS)
-            nc.vector.scalar_tensor_tensor(sums, lifted[:, :, 0, :], 0.0, second[:], ALU.max, ALU.add)
-            nc.scalar.activation(logs[:, cols], cube_sums[:, cols], ACT.Ln, scale=1.0 / D, bias=FLOOR**3)
+        def pool_pairs(group, lifted, second, pieces):
+            width = BANK_COLS // pieces
+            for c in range(0, BANK_COLS, width):
+                cols = slice(group[0] * BANK_COLS, (group[-1] + 1) * BANK_COLS)
+                sums = cube_sums[:, cols].rearrange("p (g c) -> p g c", c=BANK_COLS)[:, :, c : c + width]
+                nc.vector.scalar_tensor_tensor(
+                    sums, lifted[:, :, 0, c : c + width], 0.0, second[:, :, c : c + width], ALU.max, ALU.add
+                )
+                logs_out = logs[:, cols].rearrange("p (g c) -> p g c", c=BANK_COLS)[:, :, c : c + width]
+                nc.scalar.activation(logs_out, sums, ACT.Ln, scale=1.0 / D, bias=FLOOR**3)
+
+        shifted = keep.tile([P, V * PACK], F32, name="shifted", tag="shifted_then_result", align_bytes=64)
+
+        def shift(v0, v1):
+            nc.vector.tensor_tensor(
+                shifted[:, v0 * PACK : v1 * PACK].rearrange("p (v t) -> p v t", t=PACK),
+                logs[:, v0 * PACK : v1 * PACK].rearrange("p (v t) -> p v t", t=PACK),
+                gain_log3[:].unsqueeze(1).to_broadcast([P, v1 - v0, PACK]),
+                ALU.add,
+            )
 
         pending = []
         for group, on_scalar in BANK_GROUPS:
@@ -146,9 +162,11 @@ def tile_picked_ygem_tanh_p_kernel(tc, x_words, x_scales, w1, w2, gain, offs, ou
                 if bank == group[-1]:
                     second = clamp(group, on_scalar, lifted)
                 if pending:
-                    pool_pairs(*pending.pop())
+                    pool_pairs(*pending.pop(), 1)
             pending.append((group, lifted, second))
-        pool_pairs(*pending.pop())
+            if group[0] == 4:
+                shift(*EXP_PIECES[0])
+        pool_pairs(*pending.pop(), 2)
 
         w2_codes = keep.tile([P, N], U32, name="w2_codes", align_bytes=64)
         w2_scales = keep.tile([P, N], U8, name="w2_scales", align_bytes=64)
@@ -157,20 +175,14 @@ def tile_picked_ygem_tanh_p_kernel(tc, x_words, x_scales, w1, w2, gain, offs, ou
         nc.vector.quantize_mx(w2_codes[:].bitcast(FP8X4), w2_scales[:], w2_signed[:].rearrange("p n t -> p (n t)"))
 
         z = keep.tile([P, V * PACK], BF16, name="z", tag="sums_then_z", align_bytes=64)
-        z_codes = keep.tile([P, V], U32, name="z_codes", align_bytes=64)
+        z_codes = keep.tile([P, V], U32, name="z_codes", tag="logs_then_codes", align_bytes=64)
         z_scales = keep.tile([P, V], U8, name="z_scales", align_bytes=64)
         products = []
-        shifted = keep.tile([P, V * PACK], F32, name="shifted", tag="shifted_then_result", align_bytes=64)
-        for v0, v1 in IMAGE_CHUNKS:
-            for a in range(v0, v1, SHIFT_WIDTH):
-                b = min(a + SHIFT_WIDTH, v1)
-                nc.vector.tensor_tensor(
-                    shifted[:, a * PACK : b * PACK].rearrange("p (v t) -> p v t", t=PACK),
-                    logs[:, a * PACK : b * PACK].rearrange("p (v t) -> p v t", t=PACK),
-                    gain_log3[:].unsqueeze(1).to_broadcast([P, b - a, PACK]),
-                    ALU.add,
-                )
-            nc.scalar.activation(z[:, v0 * PACK : v1 * PACK], shifted[:, v0 * PACK : v1 * PACK], ACT.Exp, scale=1.0 / 3.0)
+        for v0, v1 in SHIFT_PIECES:
+            shift(v0, v1)
+        for v0, v1 in EXP_PIECES:
+            cols = slice(v0 * PACK, v1 * PACK)
+            nc.scalar.activation(z[:, cols], shifted[:, cols], ACT.Exp, scale=1.0 / 3.0)
         for v0, v1 in IMAGE_CHUNKS:
             nc.vector.quantize_mx(z_codes[:, v0:v1].bitcast(FP8X4), z_scales[:, v0:v1], z[:, v0 * PACK : v1 * PACK])
             product = psum.tile([P, v1 - v0], F32, name="product", tag="bank")

@@ -18,16 +18,16 @@ ACT = mybir.ActivationFunctionType
 
 P = 128
 PACK = 4
-HALF = 512
+LIST_ROWS = 16
+HALF = S // 2
 FLOOR = 0.05
 LN_SMALLEST = 2.0**-64
-BANK_ENTRIES = 128
-BANK_IMAGES = BANK_ENTRIES // D
-BANK_COLS = BANK_IMAGES * PACK
-BANK_GROUPS = (((0, 1), False), ((2, 3), True), ((4, 5), True), ((6,), False), ((7,), False))
+
+VECTOR_CLAMPED = ((0, 64, 128, 192),)
+SCALAR_CLAMPED = ((192, 256, 320, 384), (384, 448), (448, 512))
 IMAGE_CHUNKS = ((0, 256), (256, 384), (384, 448), (448, 512))
-EXP_PIECES = ((0, 16), (16, 256), (256, 384), (384, 448), (448, 512))
-SHIFT_PIECES = ((16, 256), (256, 384), (384, 448), (448, 512))
+EARLY_IMAGES = 16
+LATE_PIECES = ((EARLY_IMAGES, IMAGE_CHUNKS[0][1]),) + IMAGE_CHUNKS[1:]
 
 
 def tile_picked_ygem_tanh_p_kernel(tc, x_words, x_scales, w1, w2, gain, offs, out):
@@ -36,12 +36,12 @@ def tile_picked_ygem_tanh_p_kernel(tc, x_words, x_scales, w1, w2, gain, offs, ou
         keep = ctx.enter_context(tc.tile_pool(name="keep", bufs=1))
         psum = ctx.enter_context(tc.psum_pool(name="psum", bufs=8))
 
-        offsets = keep.tile([P, S // 16], U16, name="offsets")
+        offsets = keep.tile([P, S // LIST_ROWS], U16, name="offsets")
         gain_raw = keep.tile([P, PACK], F32, name="gain_raw")
         nc.scalar.dma_start(gain_raw[:], gain.rearrange("(p t) o -> p (t o)", t=PACK))
         scale_table = keep.tile([P, T], U8, name="scale_table", align_bytes=64)
         nc.vector.memset(scale_table[:].bitcast(I32), 0)
-        w1_raw = keep.tile([P, PACK, H], F32, name="w1_raw", tag="w1_then_w2")
+        w1_raw = keep.tile([P, PACK, H], F32, name="w1_raw")
         w1_rows = w1.rearrange("(p j) c -> p j c", j=PACK)
         nc.sync.dma_start(w1_raw[:, 0:2, :], w1_rows[:, 0:2, :])
         nc.sync.dma_start(offsets[:], offs)
@@ -49,6 +49,8 @@ def tile_picked_ygem_tanh_p_kernel(tc, x_words, x_scales, w1, w2, gain, offs, ou
         nc.sync.dma_start(w1_raw[:, 2:4, :], w1_rows[:, 2:4, :])
         word_table = keep.tile([P, T], U32, name="word_table", align_bytes=64)
         nc.sync.dma_start(word_table[:].bitcast(I32), x_words[0].rearrange("p n r -> p (n r)").bitcast(I32))
+        w2_raw = keep.tile([P, PACK, N], F32, name="w2_raw")
+        nc.sync.dma_start(w2_raw[:], w2.rearrange("(p t) n -> p t n", t=PACK))
 
         gain_abs = keep.tile([P, PACK], F32, name="gain_abs")
         nc.vector.scalar_tensor_tensor(gain_abs[:], gain_raw[:], -1.0, gain_raw[:], ALU.mult, ALU.max)
@@ -67,8 +69,8 @@ def tile_picked_ygem_tanh_p_kernel(tc, x_words, x_scales, w1, w2, gain, offs, ou
         nc.vector.memset(x_scale_rows[:].bitcast(I32), 0)
         picked_scales = keep.tile([P, S], U8, name="picked_scales", align_bytes=64)
         nc.vector.tensor_copy(picked_scales[:], scale_table[:].indirect(offsets[:]))
-        for q in range(4):
-            nc.sync.dma_start(
+        for q in range(P // 32):
+            nc.scalar.dma_start(
                 x_scale_rows[32 * q : 32 * q + 4, :].bitcast(I32),
                 picked_scales[32 * q : 32 * q + 32 : 8, :].bitcast(I32),
             )
@@ -76,20 +78,19 @@ def tile_picked_ygem_tanh_p_kernel(tc, x_words, x_scales, w1, w2, gain, offs, ou
         w1_grouped = keep.tile([P, PACK * H], BF16, name="w1_grouped", align_bytes=64)
         w1_to = w1_grouped[:].rearrange("p (t m j) -> p m t j", t=PACK, j=PACK)
         w1_from = w1_raw[:].rearrange("p j (m t) -> p m t j", t=PACK)
-        nc.vector.tensor_copy(w1_to[:, :, 0:2, :], w1_from[:, :, 0:2, :])
-        nc.scalar.copy(w1_to[:, :, 2:4, :], w1_from[:, :, 2:4, :])
+        for t in range(0, PACK, 2):
+            nc.vector.tensor_copy(w1_to[:, :, t : t + 2, :], w1_from[:, :, t : t + 2, :])
         w1_codes = keep.tile([P, H], U32, name="w1_codes", align_bytes=64)
         w1_scales = keep.tile([P, H], U8, name="w1_scales", align_bytes=64)
         nc.vector.quantize_mx(w1_codes[:].bitcast(FP8X4), w1_scales[:], w1_grouped[:])
 
         picked_words = []
-        for h in range(2):
+        for h in range(S // HALF):
             words = keep.tile([P, HALF], U32, name="picked_words%d" % h, align_bytes=64)
-            nc.vector.tensor_copy(words[:], word_table[:].indirect(offsets[:, 32 * h : 32 * (h + 1)]))
+            list_cols = slice(h * HALF // LIST_ROWS, (h + 1) * HALF // LIST_ROWS)
+            nc.vector.tensor_copy(words[:], word_table[:].indirect(offsets[:, list_cols]))
             picked_words.append(words)
 
-        w2_raw = keep.tile([P, PACK, N], F32, name="w2_raw", tag="w1_then_w2")
-        nc.sync.dma_start(w2_raw[:], w2.rearrange("(p t) n -> p t n", t=PACK))
         w2_grouped = keep.tile([P, N, PACK], BF16, name="w2_grouped", align_bytes=64)
         nc.scalar.copy(
             w2_grouped[:].rearrange("p (c i) t -> p c t i", i=4),
@@ -99,90 +100,98 @@ def tile_picked_ygem_tanh_p_kernel(tc, x_words, x_scales, w1, w2, gain, offs, ou
         cube_sums = keep.tile([P, V * PACK], F32, name="cube_sums", tag="sums_then_z", align_bytes=64)
         logs = keep.tile([P, V * PACK], F32, name="logs", tag="logs_then_codes", align_bytes=64)
 
-        def cube(bank, lifted):
-            h, first = divmod(bank * BANK_ENTRIES, HALF)
-            acc = psum.tile([P, PACK, BANK_ENTRIES], F32, name="acc", tag="bank")
+        def first_product(v0, v1):
+            entries = slice(D * v0, D * v1)
+            h, start = divmod(D * v0, HALF)
+            acc = psum.tile([P, PACK, D * (v1 - v0)], F32, name="acc", tag="bank")
             for t in range(PACK):
                 nc.tensor.matmul_mx(
                     acc[:, t, :],
                     lhsT=w1_codes[:, P * t : P * (t + 1)].bitcast(FP8X4),
                     lhsT_scale=w1_scales[:, P * t : P * (t + 1)],
-                    rhs=picked_words[h][:, first : first + BANK_ENTRIES].bitcast(FP8X4),
-                    rhs_scale=x_scale_rows[:, bank * BANK_ENTRIES : (bank + 1) * BANK_ENTRIES],
+                    rhs=picked_words[h][:, start : start + D * (v1 - v0)].bitcast(FP8X4),
+                    rhs_scale=x_scale_rows[:, entries],
                     start=True,
                     stop=True,
                 )
-            by_member = acc[:].rearrange("p t (v d) -> p d v t", d=D)
-            square = keep.tile([P, D, BANK_IMAGES, PACK], F32, name="square%d" % bank)
-            nc.scalar.activation(square[:], by_member, ACT.Square, bias=1.5 * FLOOR)
-            for d in (1, 0):
-                nc.vector.scalar_tensor_tensor(
-                    lifted[:, d, :].rearrange("p (v t) -> p v t", t=PACK),
-                    square[:, d, :, :],
-                    0.75 * FLOOR * FLOOR,
-                    by_member[:, d, :, :],
-                    ALU.add,
-                    ALU.mult,
-                )
+            return acc[:].rearrange("p t (v d) -> p v d t", d=D)
 
-        def clamp(group, on_scalar, lifted):
-            second = keep.tile([P, len(group), BANK_COLS], F32, name="second%d" % group[0])
-            if on_scalar:
-                nc.scalar.activation(second[:], lifted[:, :, 1, :], ACT.Relu)
-            else:
-                nc.vector.tensor_scalar_max(second[:], lifted[:, :, 1, :], 0.0)
-            return second
+        def lift(lifted_out, sums, name):
+            shifted_square = keep.tile(list(sums.shape), F32, name=name)
+            nc.scalar.activation(shifted_square[:], sums, ACT.Square, bias=1.5 * FLOOR)
+            nc.vector.scalar_tensor_tensor(lifted_out, shifted_square[:], 0.75 * FLOOR * FLOOR, sums, ALU.add, ALU.mult)
 
-        def pool_pairs(group, lifted, second, pieces):
-            width = BANK_COLS // pieces
-            for c in range(0, BANK_COLS, width):
-                cols = slice(group[0] * BANK_COLS, (group[-1] + 1) * BANK_COLS)
-                sums = cube_sums[:, cols].rearrange("p (g c) -> p g c", c=BANK_COLS)[:, :, c : c + width]
-                nc.vector.scalar_tensor_tensor(
-                    sums, lifted[:, :, 0, c : c + width], 0.0, second[:, :, c : c + width], ALU.max, ALU.add
-                )
-                logs_out = logs[:, cols].rearrange("p (g c) -> p g c", c=BANK_COLS)[:, :, c : c + width]
-                nc.scalar.activation(logs_out, sums, ACT.Ln, scale=1.0 / D, bias=FLOOR**3)
+        def pool_pairs(v0, v1, first, second, missing_cubes):
+            cols = slice(v0 * PACK, v1 * PACK)
+            pair_sums = cube_sums[:, cols].rearrange("p (v t) -> p v t", t=PACK)
+            nc.vector.scalar_tensor_tensor(pair_sums, first, 0.0, second, ALU.max, ALU.add)
+            nc.scalar.activation(
+                logs[:, cols], cube_sums[:, cols], ACT.Ln, scale=1.0 / D, bias=missing_cubes * FLOOR**3 / D
+            )
 
-        shifted = keep.tile([P, V * PACK], F32, name="shifted", tag="shifted_then_result", align_bytes=64)
+        gained_early = keep.tile([P, EARLY_IMAGES * PACK], F32, name="gained_early")
 
-        def shift(v0, v1):
+        def add_gain(gained_out, v0, v1):
             nc.vector.tensor_tensor(
-                shifted[:, v0 * PACK : v1 * PACK].rearrange("p (v t) -> p v t", t=PACK),
+                gained_out[:, v0 * PACK : v1 * PACK].rearrange("p (v t) -> p v t", t=PACK),
                 logs[:, v0 * PACK : v1 * PACK].rearrange("p (v t) -> p v t", t=PACK),
                 gain_log3[:].unsqueeze(1).to_broadcast([P, v1 - v0, PACK]),
                 ALU.add,
             )
 
         pending = []
-        for group, on_scalar in BANK_GROUPS:
-            lifted = keep.tile([P, len(group), D, BANK_COLS], F32, name="lifted%d" % group[0])
-            for i, bank in enumerate(group):
-                cube(bank, lifted[:, i, :, :])
-                if bank == group[-1]:
-                    second = clamp(group, on_scalar, lifted)
+        for cuts in VECTOR_CLAMPED:
+            g0, g1 = cuts[0], cuts[-1]
+            lifted = keep.tile([P, g1 - g0, D, PACK], F32, name="lifted%d" % g0)
+            second = keep.tile([P, g1 - g0, PACK], F32, name="second%d" % g0)
+            for v0, v1 in zip(cuts, cuts[1:]):
+                lift(lifted[:, v0 - g0 : v1 - g0, :, :], first_product(v0, v1), "shifted_square%d" % v0)
+            nc.vector.tensor_scalar_max(second[:], lifted[:, :, 1, :], 0.0)
+            pending.append((g0, g1, lifted[:, :, 0, :], second[:], 2))
+        for cuts in SCALAR_CLAMPED:
+            g0, g1 = cuts[0], cuts[-1]
+            first_tag = "first_then_w2" if g1 == V else "first%d" % g0
+            second_tag = "second_gained_result" if g1 == V else "second%d" % g0
+            first = keep.tile([P, g1 - g0, PACK], F32, name="first%d" % g0, tag=first_tag, align_bytes=64)
+            second = keep.tile([P, g1 - g0, PACK], F32, name="second%d" % g0, tag=second_tag, align_bytes=64)
+            clamped = keep.tile([P, g1 - g0, PACK], F32, name="clamped%d" % g0)
+            square = keep.tile([P, g1 - g0, PACK], F32, name="clamped_square%d" % g0)
+            for v0, v1 in zip(cuts, cuts[1:]):
+                sums = first_product(v0, v1)
+                nc.scalar.activation(clamped[:, v0 - g0 : v1 - g0, :], sums[:, :, 1, :], ACT.Relu)
+                lift(first[:, v0 - g0 : v1 - g0, :], sums[:, :, 0, :], "shifted_square%d" % v0)
+                if v1 == g1:
+                    nc.scalar.activation(square[:], clamped[:], ACT.Square, bias=FLOOR)
+                    nc.vector.scalar_tensor_tensor(second[:], clamped[:], FLOOR, square[:], ALU.add, ALU.mult)
                 if pending:
-                    pool_pairs(*pending.pop(), 1)
-            pending.append((group, lifted, second))
-            if group[0] == 4:
-                shift(*EXP_PIECES[0])
-        pool_pairs(*pending.pop(), 2)
+                    pool_pairs(*pending.pop())
+            pending.append((g0, g1, first[:], second[:], 1))
+        add_gain(gained_early, 0, EARLY_IMAGES)
+        v0, v1, first, second, missing_cubes = pending.pop()
+        half = (v1 - v0) // 2
+        pool_pairs(v0, v0 + half, first[:, :half, :], second[:, :half, :], missing_cubes)
+        pool_pairs(v0 + half, v1, first[:, half:, :], second[:, half:, :], missing_cubes)
 
         w2_codes = keep.tile([P, N], U32, name="w2_codes", align_bytes=64)
         w2_scales = keep.tile([P, N], U8, name="w2_scales", align_bytes=64)
-        w2_signed = keep.tile([P, N, PACK], BF16, name="w2_signed", align_bytes=64)
-        nc.vector.tensor_tensor(w2_signed[:], w2_grouped[:], gain_sign[:].unsqueeze(1).to_broadcast([P, N, PACK]), ALU.mult)
+        w2_signed = keep.tile([P, N, PACK], BF16, name="w2_signed", tag="first_then_w2", align_bytes=64)
+        signs = gain_sign[:].unsqueeze(1).to_broadcast([P, N, PACK])
+        nc.vector.tensor_tensor(w2_signed[:], w2_grouped[:], signs, ALU.mult)
         nc.vector.quantize_mx(w2_codes[:].bitcast(FP8X4), w2_scales[:], w2_signed[:].rearrange("p n t -> p (n t)"))
 
         z = keep.tile([P, V * PACK], BF16, name="z", tag="sums_then_z", align_bytes=64)
         z_codes = keep.tile([P, V], U32, name="z_codes", tag="logs_then_codes", align_bytes=64)
         z_scales = keep.tile([P, V], U8, name="z_scales", align_bytes=64)
-        products = []
-        for v0, v1 in SHIFT_PIECES:
-            shift(v0, v1)
-        for v0, v1 in EXP_PIECES:
+        gained = keep.tile([P, V * PACK], F32, name="gained", tag="second_gained_result", align_bytes=64)
+        for v0, v1 in LATE_PIECES:
+            add_gain(gained, v0, v1)
+
+        nc.scalar.activation(z[:, : EARLY_IMAGES * PACK], gained_early[:], ACT.Exp, scale=1.0 / 3.0)
+        for v0, v1 in LATE_PIECES:
             cols = slice(v0 * PACK, v1 * PACK)
-            nc.scalar.activation(z[:, cols], shifted[:, cols], ACT.Exp, scale=1.0 / 3.0)
+            nc.scalar.activation(z[:, cols], gained[:, cols], ACT.Exp, scale=1.0 / 3.0)
+
+        whitened = []
         for v0, v1 in IMAGE_CHUNKS:
             nc.vector.quantize_mx(z_codes[:, v0:v1].bitcast(FP8X4), z_scales[:, v0:v1], z[:, v0 * PACK : v1 * PACK])
             product = psum.tile([P, v1 - v0], F32, name="product", tag="bank")
@@ -195,9 +204,9 @@ def tile_picked_ygem_tanh_p_kernel(tc, x_words, x_scales, w1, w2, gain, offs, ou
                 start=True,
                 stop=True,
             )
-            products.append(product)
-        result = keep.tile([P, V], F32, name="result", tag="shifted_then_result", align_bytes=64)
-        for (v0, v1), product in zip(IMAGE_CHUNKS, products):
+            whitened.append(product)
+        result = keep.tile([P, V], F32, name="result", tag="second_gained_result", align_bytes=64)
+        for (v0, v1), product in zip(IMAGE_CHUNKS, whitened):
             nc.scalar.activation(result[:, v0:v1], product[:], ACT.Tanh)
             queue = nc.scalar if v1 == V else nc.sync
             queue.dma_start(out[:, v0:v1], result[:, v0:v1])

@@ -21,10 +21,11 @@ PACK = 4
 LIST_ROWS = 16
 HALF = S // 2
 FLOOR = 0.05
+F32_LARGEST = (2.0 - 2.0**-23) * 2.0**127
 LN_SMALLEST = 2.0**-64
 
-VECTOR_CLAMPED = ((0, 64, 128, 192),)
-SCALAR_CLAMPED = ((192, 256, 320, 384), (384, 448), (448, 512))
+GPSIMD_CLAMPED = ((0, 64, 128), (128, 192, 256), (256, 320))
+SCALAR_CLAMPED = ((320, 384), (384, 448), (448, 512))
 IMAGE_CHUNKS = ((0, 256), (256, 384), (384, 448), (448, 512))
 EARLY_IMAGES = 16
 LATE_PIECES = ((EARLY_IMAGES, IMAGE_CHUNKS[0][1]),) + IMAGE_CHUNKS[1:]
@@ -140,13 +141,16 @@ def tile_picked_ygem_tanh_p_kernel(tc, x_words, x_scales, w1, w2, gain, offs, ou
             )
 
         pending = []
-        for cuts in VECTOR_CLAMPED:
+        for cuts in GPSIMD_CLAMPED:
             g0, g1 = cuts[0], cuts[-1]
             lifted = keep.tile([P, g1 - g0, D, PACK], F32, name="lifted%d" % g0)
             second = keep.tile([P, g1 - g0, PACK], F32, name="second%d" % g0)
             for v0, v1 in zip(cuts, cuts[1:]):
                 lift(lifted[:, v0 - g0 : v1 - g0, :, :], first_product(v0, v1), "shifted_square%d" % v0)
-            nc.vector.tensor_scalar_max(second[:], lifted[:, :, 1, :], 0.0)
+                if v1 == g1:
+                    nc.gpsimd.tensor_scalar(second[:], lifted[:, :, 1, :], F32_LARGEST, 0.0, ALU.min, ALU.max)
+                if pending:
+                    pool_pairs(*pending.pop())
             pending.append((g0, g1, lifted[:, :, 0, :], second[:], 2))
         for cuts in SCALAR_CLAMPED:
             g0, g1 = cuts[0], cuts[-1]

from contextlib import ExitStack

import concourse.mybir as mybir

K, T, S, H, N, D = 512, 4096, 1024, 512, 128, 2
V = S // D
FLOPS = 2 * K * H * S + 2 * H * N * V

F32 = mybir.dt.float32
BF16 = mybir.dt.bfloat16
I32 = mybir.dt.int32
U32 = mybir.dt.uint32
U16 = mybir.dt.uint16
U8 = mybir.dt.uint8
FP8X4 = mybir.dt.float8_e4m3fn_x4
ALU = mybir.AluOpType
ACT = mybir.ActivationFunctionType

P = 128
PACK = 4
LIST_ROWS = 16
HALF = S // 2
FLOOR = 0.05
F32_LARGEST = (2.0 - 2.0**-23) * 2.0**127
LN_SMALLEST = 2.0**-64

GPSIMD_CLAMPED = ((0, 64, 128), (128, 192, 256), (256, 320))
SCALAR_CLAMPED = ((320, 384), (384, 448), (448, 512))
IMAGE_CHUNKS = ((0, 256), (256, 384), (384, 448), (448, 512))
EARLY_IMAGES = 16
LATE_PIECES = ((EARLY_IMAGES, IMAGE_CHUNKS[0][1]),) + IMAGE_CHUNKS[1:]


def tile_picked_ygem_tanh_p_kernel(tc, x_words, x_scales, w1, w2, gain, offs, out):
    nc = tc.nc
    with ExitStack() as ctx:
        keep = ctx.enter_context(tc.tile_pool(name="keep", bufs=1))
        psum = ctx.enter_context(tc.psum_pool(name="psum", bufs=8))

        offsets = keep.tile([P, S // LIST_ROWS], U16, name="offsets")
        gain_raw = keep.tile([P, PACK], F32, name="gain_raw")
        nc.scalar.dma_start(gain_raw[:], gain.rearrange("(p t) o -> p (t o)", t=PACK))
        scale_table = keep.tile([P, T], U8, name="scale_table", align_bytes=64)
        nc.vector.memset(scale_table[:].bitcast(I32), 0)
        w1_raw = keep.tile([P, PACK, H], F32, name="w1_raw")
        w1_rows = w1.rearrange("(p j) c -> p j c", j=PACK)
        nc.sync.dma_start(w1_raw[:, 0:2, :], w1_rows[:, 0:2, :])
        nc.sync.dma_start(offsets[:], offs)
        nc.sync.dma_start(scale_table[0:P:8, :].bitcast(I32), x_scales[0].bitcast(I32))
        nc.sync.dma_start(w1_raw[:, 2:4, :], w1_rows[:, 2:4, :])
        word_table = keep.tile([P, T], U32, name="word_table", align_bytes=64)
        nc.sync.dma_start(word_table[:].bitcast(I32), x_words[0].rearrange("p n r -> p (n r)").bitcast(I32))
        w2_raw = keep.tile([P, PACK, N], F32, name="w2_raw")
        nc.sync.dma_start(w2_raw[:], w2.rearrange("(p t) n -> p t n", t=PACK))

        gain_abs = keep.tile([P, PACK], F32, name="gain_abs")
        nc.vector.scalar_tensor_tensor(gain_abs[:], gain_raw[:], -1.0, gain_raw[:], ALU.mult, ALU.max)
        gain_clamped = keep.tile([P, PACK], F32, name="gain_clamped")
        nc.vector.tensor_scalar_max(gain_clamped[:], gain_abs[:], LN_SMALLEST)
        gain_log = keep.tile([P, PACK], F32, name="gain_log")
        nc.scalar.activation(gain_log[:], gain_clamped[:], ACT.Ln)
        gain_log3 = keep.tile([P, PACK], F32, name="gain_log3")
        nc.vector.tensor_scalar(gain_log3[:], gain_log[:], 3.0, None, ALU.mult)
        gain_step = keep.tile([P, PACK], F32, name="gain_step")
        nc.vector.tensor_scalar(gain_step[:], gain_raw[:], 0.0, 2.0, ALU.is_ge, ALU.mult)
        gain_sign = keep.tile([P, PACK], BF16, name="gain_sign")
        nc.vector.tensor_scalar(gain_sign[:], gain_step[:], -1.0, None, ALU.add)

        x_scale_rows = keep.tile([P, S], U8, name="x_scale_rows", align_bytes=64)
        nc.vector.memset(x_scale_rows[:].bitcast(I32), 0)
        picked_scales = keep.tile([P, S], U8, name="picked_scales", align_bytes=64)
        nc.vector.tensor_copy(picked_scales[:], scale_table[:].indirect(offsets[:]))
        for q in range(P // 32):
            nc.scalar.dma_start(
                x_scale_rows[32 * q : 32 * q + 4, :].bitcast(I32),
                picked_scales[32 * q : 32 * q + 32 : 8, :].bitcast(I32),
            )

        w1_grouped = keep.tile([P, PACK * H], BF16, name="w1_grouped", align_bytes=64)
        w1_to = w1_grouped[:].rearrange("p (t m j) -> p m t j", t=PACK, j=PACK)
        w1_from = w1_raw[:].rearrange("p j (m t) -> p m t j", t=PACK)
        for t in range(0, PACK, 2):
            nc.vector.tensor_copy(w1_to[:, :, t : t + 2, :], w1_from[:, :, t : t + 2, :])
        w1_codes = keep.tile([P, H], U32, name="w1_codes", align_bytes=64)
        w1_scales = keep.tile([P, H], U8, name="w1_scales", align_bytes=64)
        nc.vector.quantize_mx(w1_codes[:].bitcast(FP8X4), w1_scales[:], w1_grouped[:])

        picked_words = []
        for h in range(S // HALF):
            words = keep.tile([P, HALF], U32, name="picked_words%d" % h, align_bytes=64)
            list_cols = slice(h * HALF // LIST_ROWS, (h + 1) * HALF // LIST_ROWS)
            nc.vector.tensor_copy(words[:], word_table[:].indirect(offsets[:, list_cols]))
            picked_words.append(words)

        w2_grouped = keep.tile([P, N, PACK], BF16, name="w2_grouped", align_bytes=64)
        nc.scalar.copy(
            w2_grouped[:].rearrange("p (c i) t -> p c t i", i=4),
            w2_raw[:].rearrange("p t (c i) -> p c t i", i=4),
        )

        cube_sums = keep.tile([P, V * PACK], F32, name="cube_sums", tag="sums_then_z", align_bytes=64)
        logs = keep.tile([P, V * PACK], F32, name="logs", tag="logs_then_codes", align_bytes=64)

        def first_product(v0, v1):
            entries = slice(D * v0, D * v1)
            h, start = divmod(D * v0, HALF)
            acc = psum.tile([P, PACK, D * (v1 - v0)], F32, name="acc", tag="bank")
            for t in range(PACK):
                nc.tensor.matmul_mx(
                    acc[:, t, :],
                    lhsT=w1_codes[:, P * t : P * (t + 1)].bitcast(FP8X4),
                    lhsT_scale=w1_scales[:, P * t : P * (t + 1)],
                    rhs=picked_words[h][:, start : start + D * (v1 - v0)].bitcast(FP8X4),
                    rhs_scale=x_scale_rows[:, entries],
                    start=True,
                    stop=True,
                )
            return acc[:].rearrange("p t (v d) -> p v d t", d=D)

        def lift(lifted_out, sums, name):
            shifted_square = keep.tile(list(sums.shape), F32, name=name)
            nc.scalar.activation(shifted_square[:], sums, ACT.Square, bias=1.5 * FLOOR)
            nc.vector.scalar_tensor_tensor(lifted_out, shifted_square[:], 0.75 * FLOOR * FLOOR, sums, ALU.add, ALU.mult)

        def pool_pairs(v0, v1, first, second, missing_cubes):
            cols = slice(v0 * PACK, v1 * PACK)
            pair_sums = cube_sums[:, cols].rearrange("p (v t) -> p v t", t=PACK)
            nc.vector.scalar_tensor_tensor(pair_sums, first, 0.0, second, ALU.max, ALU.add)
            nc.scalar.activation(
                logs[:, cols], cube_sums[:, cols], ACT.Ln, scale=1.0 / D, bias=missing_cubes * FLOOR**3 / D
            )

        gained_early = keep.tile([P, EARLY_IMAGES * PACK], F32, name="gained_early")

        def add_gain(gained_out, v0, v1):
            nc.vector.tensor_tensor(
                gained_out[:, v0 * PACK : v1 * PACK].rearrange("p (v t) -> p v t", t=PACK),
                logs[:, v0 * PACK : v1 * PACK].rearrange("p (v t) -> p v t", t=PACK),
                gain_log3[:].unsqueeze(1).to_broadcast([P, v1 - v0, PACK]),
                ALU.add,
            )

        pending = []
        for cuts in GPSIMD_CLAMPED:
            g0, g1 = cuts[0], cuts[-1]
            lifted = keep.tile([P, g1 - g0, D, PACK], F32, name="lifted%d" % g0)
            second = keep.tile([P, g1 - g0, PACK], F32, name="second%d" % g0)
            for v0, v1 in zip(cuts, cuts[1:]):
                lift(lifted[:, v0 - g0 : v1 - g0, :, :], first_product(v0, v1), "shifted_square%d" % v0)
                if v1 == g1:
                    nc.gpsimd.tensor_scalar(second[:], lifted[:, :, 1, :], F32_LARGEST, 0.0, ALU.min, ALU.max)
                if pending:
                    pool_pairs(*pending.pop())
            pending.append((g0, g1, lifted[:, :, 0, :], second[:], 2))
        for cuts in SCALAR_CLAMPED:
            g0, g1 = cuts[0], cuts[-1]
            first_tag = "first_then_w2" if g1 == V else "first%d" % g0
            second_tag = "second_gained_result" if g1 == V else "second%d" % g0
            first = keep.tile([P, g1 - g0, PACK], F32, name="first%d" % g0, tag=first_tag, align_bytes=64)
            second = keep.tile([P, g1 - g0, PACK], F32, name="second%d" % g0, tag=second_tag, align_bytes=64)
            clamped = keep.tile([P, g1 - g0, PACK], F32, name="clamped%d" % g0)
            square = keep.tile([P, g1 - g0, PACK], F32, name="clamped_square%d" % g0)
            for v0, v1 in zip(cuts, cuts[1:]):
                sums = first_product(v0, v1)
                nc.scalar.activation(clamped[:, v0 - g0 : v1 - g0, :], sums[:, :, 1, :], ACT.Relu)
                lift(first[:, v0 - g0 : v1 - g0, :], sums[:, :, 0, :], "shifted_square%d" % v0)
                if v1 == g1:
                    nc.scalar.activation(square[:], clamped[:], ACT.Square, bias=FLOOR)
                    nc.vector.scalar_tensor_tensor(second[:], clamped[:], FLOOR, square[:], ALU.add, ALU.mult)
                if pending:
                    pool_pairs(*pending.pop())
            pending.append((g0, g1, first[:], second[:], 1))
        add_gain(gained_early, 0, EARLY_IMAGES)
        v0, v1, first, second, missing_cubes = pending.pop()
        half = (v1 - v0) // 2
        pool_pairs(v0, v0 + half, first[:, :half, :], second[:, :half, :], missing_cubes)
        pool_pairs(v0 + half, v1, first[:, half:, :], second[:, half:, :], missing_cubes)

        w2_codes = keep.tile([P, N], U32, name="w2_codes", align_bytes=64)
        w2_scales = keep.tile([P, N], U8, name="w2_scales", align_bytes=64)
        w2_signed = keep.tile([P, N, PACK], BF16, name="w2_signed", tag="first_then_w2", align_bytes=64)
        signs = gain_sign[:].unsqueeze(1).to_broadcast([P, N, PACK])
        nc.vector.tensor_tensor(w2_signed[:], w2_grouped[:], signs, ALU.mult)
        nc.vector.quantize_mx(w2_codes[:].bitcast(FP8X4), w2_scales[:], w2_signed[:].rearrange("p n t -> p (n t)"))

        z = keep.tile([P, V * PACK], BF16, name="z", tag="sums_then_z", align_bytes=64)
        z_codes = keep.tile([P, V], U32, name="z_codes", tag="logs_then_codes", align_bytes=64)
        z_scales = keep.tile([P, V], U8, name="z_scales", align_bytes=64)
        gained = keep.tile([P, V * PACK], F32, name="gained", tag="second_gained_result", align_bytes=64)
        for v0, v1 in LATE_PIECES:
            add_gain(gained, v0, v1)

        nc.scalar.activation(z[:, : EARLY_IMAGES * PACK], gained_early[:], ACT.Exp, scale=1.0 / 3.0)
        for v0, v1 in LATE_PIECES:
            cols = slice(v0 * PACK, v1 * PACK)
            nc.scalar.activation(z[:, cols], gained[:, cols], ACT.Exp, scale=1.0 / 3.0)

        whitened = []
        for v0, v1 in IMAGE_CHUNKS:
            nc.vector.quantize_mx(z_codes[:, v0:v1].bitcast(FP8X4), z_scales[:, v0:v1], z[:, v0 * PACK : v1 * PACK])
            product = psum.tile([P, v1 - v0], F32, name="product", tag="bank")
            nc.tensor.matmul_mx(
                product[:],
                lhsT=w2_codes[:].bitcast(FP8X4),
                lhsT_scale=w2_scales[:],
                rhs=z_codes[:, v0:v1].bitcast(FP8X4),
                rhs_scale=z_scales[:, v0:v1],
                start=True,
                stop=True,
            )
            whitened.append(product)
        result = keep.tile([P, V], F32, name="result", tag="second_gained_result", align_bytes=64)
        for (v0, v1), product in zip(IMAGE_CHUNKS, whitened):
            nc.scalar.activation(result[:, v0:v1], product[:], ACT.Tanh)
            queue = nc.scalar if v1 == V else nc.sync
            queue.dma_start(out[:, v0:v1], result[:, v0:v1])
